import numpy as np
import ml_dtypes


def mxq(x, axis, fmt="e4m3"):
    dtype, down = {"e4m3": (ml_dtypes.float8_e4m3fn, 7), "e5m2": (ml_dtypes.float8_e5m2, 14)}[fmt]
    v = np.moveaxis(np.asarray(x, np.float32).astype(ml_dtypes.bfloat16).astype(np.float64), axis, -1)
    blocks = v.reshape(v.shape[:-1] + (-1, 32))
    amax = np.abs(blocks).max(-1, keepdims=True)
    byte = np.maximum(np.where(amax > 0, np.frexp(amax)[1] - 1 + 127, 0) - down, 1)
    scale = np.exp2(byte - 127.0)
    codes = (blocks / scale).astype(np.float32).astype(dtype).astype(np.float64)
    return np.moveaxis((codes * scale).reshape(v.shape), -1, axis)


WIDE = False


def mx_kscale(k):
    if not WIDE:
        return np.ones(k)
    levels = np.array([10, -10, 5, -5, 0])
    if k % 512:
        return np.exp2(np.random.permutation(np.resize(levels, k // 32))).repeat(32)
    a = np.empty((k // 512, 16))
    for p in range(k // 512):
        a[p, :8] = np.random.permutation(np.resize(levels, 8))
        for g in range(8):
            far = levels[np.abs(levels - a[p, g]) >= 10]
            a[p, g + 8] = far[np.random.randint(len(far))]
    return np.exp2(a.ravel()).repeat(32)


def f64(x):
    return np.asarray(x).astype(np.float64)


def striped8(idx):
    return np.concatenate([v.reshape(-1, 16).T for v in idx]).astype(np.uint16)


def unstriped8(offs):
    return np.stack([offs[16 * g:16 * g + 16].T.reshape(-1) for g in range(8)]).astype(np.int64)


def silu(v):
    return v / (1.0 + np.exp(-np.maximum(v, -700.0)))


K, M, T, S = 1024, 1024, 2048, 512


def setup_inputs():
    n = np.random.standard_normal
    s = mx_kscale(K)[:, None]
    return {
        "xT": (n((K, T)) * s).astype(np.float32),
        "w": (n((K, M)) / np.sqrt(K) / s).astype(np.float32),
        "wgt": np.repeat(np.random.uniform(0.5, 2.0, (8, S)), 16, axis=0).astype(np.float32),
        "b": (0.3 * n(1024)).astype(np.float32),
        "offs": striped8(np.stack([np.random.permutation(T)[:S] for _ in range(8)])),
    }


def reference(xT, w, wgt, b, offs):
    idx = unstriped8(offs)
    group = np.arange(K) % 512 // 64
    xg = f64(wgt)[np.arange(K) // 4 % 128] * f64(xT)[np.arange(K)[:, None], idx[group]]
    xT_ = mxq(xg, 0, "e4m3")
    w_ = mxq(f64(w), 0, "e4m3")
    y = w_.T @ xT_
    return silu(y + f64(b)[:, None])

@@ -1,0 +1,161 @@
+from contextlib import ExitStack
+
+import concourse.mybir as mybir
+
+K, M, T, S = 1024, 1024, 2048, 512
+FLOPS = 2 * K * M * S
+
+F32 = mybir.dt.float32
+BF16 = mybir.dt.bfloat16
+I16 = mybir.dt.uint16
+U32 = mybir.dt.uint32
+U8 = mybir.dt.uint8
+FP8X4 = mybir.dt.float8_e4m3fn_x4
+MULT = mybir.AluOpType.mult
+SILU = mybir.ActivationFunctionType.Silu
+
+P = 128
+PACK = 4
+PASSES = K // (P * PACK)
+HALF = S // 2
+N_TILES = M // P
+
+
+def tile_list_heads_silu_kernel(tc, xT, w, wgt, b, offs, out):
+    nc = tc.nc
+    with ExitStack() as ctx:
+        keep = ctx.enter_context(tc.tile_pool(name="keep", bufs=1))
+        psum = ctx.enter_context(tc.psum_pool(name="psum", bufs=1))
+
+        offsets = keep.tile([P, S // 16], I16, name="offsets")
+        nc.sync.dma_start(offsets[:], offs)
+
+        x_rows = xT.rearrange("(a p i) t -> a i p t", p=P, i=PACK)
+        w_rows = w.rearrange("(a p i) n -> a p i n", p=P, i=PACK)
+
+        w_raw = {}
+
+        def load_w(a, n0, width):
+            raw = keep.tile([P, PACK, width], F32, name=f"w_raw_{a}_{n0}")
+            nc.sync.dma_start(raw[:], w_rows[a][:, :, n0 : n0 + width])
+            w_raw[(a, n0)] = raw
+
+        x_planes = {}
+
+        def load_x(a, i):
+            plane = keep.tile([P, T], F32, name=f"x_{a}_{i}")
+            nc.sync.dma_start(plane[:], x_rows[a, i])
+            x_planes[(a, i)] = plane
+
+        load_w(0, 0, 1024)
+        weights = keep.tile([P, S], F32, name="weights")
+        nc.sync.dma_start(weights[:], wgt)
+        load_w(1, 0, 256)
+        for a in range(PASSES):
+            for i in range(PACK):
+                load_x(a, i)
+        for n0 in (256, 512, 768):
+            load_w(1, n0, 256)
+
+        b_rows = keep.tile([P, 32], F32, name="b_rows", align_bytes=64)
+        bias = keep.tile([P, 32], F32, name="bias", align_bytes=64)
+        nc.vector.memset(b_rows[:], 0.0)
+        b_view = b.rearrange("(c q r) -> q c r", q=4, r=32)
+        for q in range(4):
+            nc.gpsimd.dma_start(b_rows[32 * q : 32 * q + N_TILES, :], b_view[q])
+        warm = keep.tile([P, 1], F32, name="warm")
+        nc.vector.memset(warm[:], 0.0)
+        nc.scalar.activation(warm[:], warm[:], SILU)
+        nc.vector.transpose(bias[:], b_rows[:])
+
+        def interleave(copy, grouped, source):
+            copy(
+                out=grouped[:].rearrange("p (c e) i -> p c i e", e=4),
+                in_=source.rearrange("p i (c e) -> p c i e", e=4),
+            )
+
+        def quantize(grouped, codes, scales):
+            nc.vector.quantize_mx(
+                out=codes.bitcast(FP8X4), scales=scales, in_=grouped[:].rearrange("p n i -> p (n i)")
+            )
+
+        w_tiles = {}
+
+        def group_w(copy, a, raw_n0, n0, width):
+            grouped = keep.tile([P, width, PACK], BF16, name=f"w_grouped_{a}_{n0}", align_bytes=64)
+            start = n0 - raw_n0
+            interleave(copy, grouped, w_raw[(a, raw_n0)][:, :, start : start + width])
+            return grouped
+
+        def quantize_w(grouped, a, n0, width):
+            codes = keep.tile([P, width], U32, name=f"w_codes_{a}_{n0}", align_bytes=64)
+            scales = keep.tile([P, width], U8, name=f"w_scales_{a}_{n0}", align_bytes=64)
+            quantize(grouped, codes[:], scales[:])
+            for c in range(0, width, P):
+                w_tiles[(a, (n0 + c) // P)] = (codes[:, c : c + P], scales[:, c : c + P])
+
+        low = group_w(nc.scalar.copy, 0, 0, 0, 512)
+        high = group_w(nc.vector.tensor_copy, 0, 0, 512, 512)
+        first = group_w(nc.scalar.copy, 1, 0, 0, 256)
+        quantize_w(low, 0, 0, 512)
+        quantize_w(high, 0, 512, 512)
+        quantize_w(first, 1, 0, 256)
+
+        acc = [psum.tile([P, S], F32, name=f"acc_{m}") for m in range(N_TILES)]
+        x_codes = [keep.tile([P, S], U32, name=f"x_codes_{a}", align_bytes=64) for a in range(PASSES)]
+        x_scales = [keep.tile([P, S], U8, name=f"x_scales_{a}", align_bytes=64) for a in range(PASSES)]
+        picked = {}
+
+        def gather(a, i, h):
+            nc.vector.tensor_tensor(
+                picked[(a, h)][:, i, :],
+                x_planes[(a, i)][:].indirect(offsets[:, h * (HALF // 16) : (h + 1) * (HALF // 16)]),
+                weights[:, h * HALF : (h + 1) * HALF],
+                MULT,
+            )
+
+        def multiply(a, m):
+            codes, scales = w_tiles[(a, m)]
+            nc.tensor.matmul_mx(
+                out=acc[m][:],
+                lhsT=codes.bitcast(FP8X4),
+                lhsT_scale=scales,
+                rhs=x_codes[a][:].bitcast(FP8X4),
+                rhs_scale=x_scales[a][:],
+                start=(a == 0),
+                stop=(a == PASSES - 1),
+            )
+
+        for a in range(PASSES):
+            for h in range(2):
+                picked[(a, h)] = keep.tile([P, PACK, HALF], F32, name=f"picked_{a}_{h}")
+            for i in range(PACK):
+                for h in range(2):
+                    gather(a, i, h)
+            x_grouped = []
+            for h in range(2):
+                grouped = keep.tile([P, HALF, PACK], BF16, name=f"x_grouped_{a}_{h}", align_bytes=64)
+                copy = nc.vector.tensor_copy if a == 1 and h == 1 else nc.scalar.copy
+                interleave(copy, grouped, picked[(a, h)][:])
+                x_grouped.append(grouped)
+            for h in range(2):
+                cols = slice(h * HALF, (h + 1) * HALF)
+                quantize(x_grouped[h], x_codes[a][:, cols], x_scales[a][:, cols])
+            if a == 0:
+                for m in range(N_TILES):
+                    multiply(a, m)
+
+        def finish(m):
+            multiply(1, m)
+            result = keep.tile([P, S], F32, name=f"result_{m}")
+            nc.scalar.activation(result[:], acc[m][:], SILU, bias=bias[:, m : m + 1])
+            nc.sync.dma_start(out[m * P : (m + 1) * P, :], result[:])
+
+        finish(0)
+        finish(1)
+        for n0 in (256, 512, 768):
+            pieces = [group_w(nc.vector.tensor_copy, 1, n0, n0 + c, P) for c in (0, P)]
+            for c in (0, 1):
+                quantize_w(pieces[c], 1, n0 + c * P, P)
+            finish(n0 // P)
+            finish(n0 // P + 1)

@@ -7,7 +7,7 @@ FLOPS = 2 * K * M * S
 
 F32 = mybir.dt.float32
 BF16 = mybir.dt.bfloat16
-I16 = mybir.dt.uint16
+U16 = mybir.dt.uint16
 U32 = mybir.dt.uint32
 U8 = mybir.dt.uint8
 FP8X4 = mybir.dt.float8_e4m3fn_x4
@@ -27,7 +27,7 @@ def tile_list_heads_silu_kernel(tc, xT, w, wgt, b, offs, out):
         keep = ctx.enter_context(tc.tile_pool(name="keep", bufs=1))
         psum = ctx.enter_context(tc.psum_pool(name="psum", bufs=1))
 
-        offsets = keep.tile([P, S // 16], I16, name="offsets")
+        offsets = keep.tile([P, S // 16], U16, name="offsets")
         nc.sync.dma_start(offsets[:], offs)
 
         x_rows = xT.rearrange("(a p i) t -> a i p t", p=P, i=PACK)
@@ -47,26 +47,26 @@ def tile_list_heads_silu_kernel(tc, xT, w, wgt, b, offs, out):
             nc.sync.dma_start(plane[:], x_rows[a, i])
             x_planes[(a, i)] = plane
 
-        load_w(0, 0, 1024)
-        weights = keep.tile([P, S], F32, name="weights")
-        nc.sync.dma_start(weights[:], wgt)
-        load_w(1, 0, 256)
-        for a in range(PASSES):
-            for i in range(PACK):
-                load_x(a, i)
-        for n0 in (256, 512, 768):
-            load_w(1, n0, 256)
+        load_w(0, 0, 768)
 
         b_rows = keep.tile([P, 32], F32, name="b_rows", align_bytes=64)
         bias = keep.tile([P, 32], F32, name="bias", align_bytes=64)
         nc.vector.memset(b_rows[:], 0.0)
         b_view = b.rearrange("(c q r) -> q c r", q=4, r=32)
         for q in range(4):
-            nc.gpsimd.dma_start(b_rows[32 * q : 32 * q + N_TILES, :], b_view[q])
+            nc.sync.dma_start(b_rows[32 * q : 32 * q + N_TILES, :], b_view[q])
+        weights = keep.tile([P, S], F32, name="weights")
+        nc.sync.dma_start(weights[:], wgt)
+        load_w(1, 0, 256)
+        for a in range(PASSES):
+            for i in range(PACK):
+                load_x(a, i)
+        for a, n0 in ((1, 256), (0, 768), (1, 512), (1, 768)):
+            load_w(a, n0, 256)
+
         warm = keep.tile([P, 1], F32, name="warm")
         nc.vector.memset(warm[:], 0.0)
         nc.scalar.activation(warm[:], warm[:], SILU)
-        nc.vector.transpose(bias[:], b_rows[:])
 
         def interleave(copy, grouped, source):
             copy(
@@ -95,11 +95,13 @@ def tile_list_heads_silu_kernel(tc, xT, w, wgt, b, offs, out):
                 w_tiles[(a, (n0 + c) // P)] = (codes[:, c : c + P], scales[:, c : c + P])
 
         low = group_w(nc.scalar.copy, 0, 0, 0, 512)
-        high = group_w(nc.vector.tensor_copy, 0, 0, 512, 512)
+        high = group_w(nc.vector.tensor_copy, 0, 0, 512, 256)
         first = group_w(nc.scalar.copy, 1, 0, 0, 256)
         quantize_w(low, 0, 0, 512)
-        quantize_w(high, 0, 512, 512)
+        quantize_w(high, 0, 512, 256)
         quantize_w(first, 1, 0, 256)
+
+        nc.vector.transpose(bias[:], b_rows[:])
 
         acc = [psum.tile([P, S], F32, name=f"acc_{m}") for m in range(N_TILES)]
         x_codes = [keep.tile([P, S], U32, name=f"x_codes_{a}", align_bytes=64) for a in range(PASSES)]
@@ -142,7 +144,7 @@ def tile_list_heads_silu_kernel(tc, xT, w, wgt, b, offs, out):
                 cols = slice(h * HALF, (h + 1) * HALF)
                 quantize(x_grouped[h], x_codes[a][:, cols], x_scales[a][:, cols])
             if a == 0:
-                for m in range(N_TILES):
+                for m in range(6):
                     multiply(a, m)
 
         def finish(m):
@@ -151,11 +153,21 @@ def tile_list_heads_silu_kernel(tc, xT, w, wgt, b, offs, out):
             nc.scalar.activation(result[:], acc[m][:], SILU, bias=bias[:, m : m + 1])
             nc.sync.dma_start(out[m * P : (m + 1) * P, :], result[:])
 
+        second = group_w(nc.scalar.copy, 1, 256, 256, 256)
         finish(0)
         finish(1)
-        for n0 in (256, 512, 768):
+        quantize_w(second, 1, 256, 256)
+        finish(2)
+        finish(3)
+        last = group_w(nc.vector.tensor_copy, 0, 768, 768, 256)
+        for n0 in (512, 768):
             pieces = [group_w(nc.vector.tensor_copy, 1, n0, n0 + c, P) for c in (0, P)]
+            if n0 == 512:
+                quantize_w(last, 0, 768, 256)
             for c in (0, 1):
                 quantize_w(pieces[c], 1, n0 + c * P, P)
+            if n0 == 768:
+                multiply(0, 6)
+                multiply(0, 7)
             finish(n0 // P)
             finish(n0 // P + 1)

@@ -47,7 +47,7 @@ def tile_list_heads_silu_kernel(tc, xT, w, wgt, b, offs, out):
             nc.sync.dma_start(plane[:], x_rows[a, i])
             x_planes[(a, i)] = plane
 
-        load_w(0, 0, 768)
+        load_w(0, 0, 512)
 
         b_rows = keep.tile([P, 32], F32, name="b_rows", align_bytes=64)
         bias = keep.tile([P, 32], F32, name="bias", align_bytes=64)
@@ -61,8 +61,8 @@ def tile_list_heads_silu_kernel(tc, xT, w, wgt, b, offs, out):
         for a in range(PASSES):
             for i in range(PACK):
                 load_x(a, i)
-        for a, n0 in ((1, 256), (0, 768), (1, 512), (1, 768)):
-            load_w(a, n0, 256)
+        for a, n0, width in ((1, 256, 256), (0, 512, 256), (1, 512, 256), (0, 768, 256), (1, 768, 128), (1, 896, 128)):
+            load_w(a, n0, width)
 
         warm = keep.tile([P, 1], F32, name="warm")
         nc.vector.memset(warm[:], 0.0)
@@ -95,10 +95,8 @@ def tile_list_heads_silu_kernel(tc, xT, w, wgt, b, offs, out):
                 w_tiles[(a, (n0 + c) // P)] = (codes[:, c : c + P], scales[:, c : c + P])
 
         low = group_w(nc.scalar.copy, 0, 0, 0, 512)
-        high = group_w(nc.vector.tensor_copy, 0, 0, 512, 256)
         first = group_w(nc.scalar.copy, 1, 0, 0, 256)
         quantize_w(low, 0, 0, 512)
-        quantize_w(high, 0, 512, 256)
         quantize_w(first, 1, 0, 256)
 
         nc.vector.transpose(bias[:], b_rows[:])
@@ -131,20 +129,26 @@ def tile_list_heads_silu_kernel(tc, xT, w, wgt, b, offs, out):
         for a in range(PASSES):
             for h in range(2):
                 picked[(a, h)] = keep.tile([P, PACK, HALF], F32, name=f"picked_{a}_{h}")
+            x_grouped = [
+                keep.tile([P, HALF, PACK], BF16, name=f"x_grouped_{a}_{h}", align_bytes=64) for h in range(2)
+            ]
             for i in range(PACK):
                 for h in range(2):
                     gather(a, i, h)
-            x_grouped = []
-            for h in range(2):
-                grouped = keep.tile([P, HALF, PACK], BF16, name=f"x_grouped_{a}_{h}", align_bytes=64)
-                copy = nc.vector.tensor_copy if a == 1 and h == 1 else nc.scalar.copy
-                interleave(copy, grouped, picked[(a, h)][:])
-                x_grouped.append(grouped)
+                if a == 1 and i % 2 == 1:
+                    for h, copy in ((0, nc.scalar.copy), (1, nc.vector.tensor_copy)):
+                        copy(
+                            out=x_grouped[h][:, :, i - 1 : i + 1],
+                            in_=picked[(a, h)][:, i - 1 : i + 1, :].rearrange("p i j -> p j i"),
+                        )
+            if a == 0:
+                for h in range(2):
+                    interleave(nc.scalar.copy, x_grouped[h], picked[(a, h)][:])
             for h in range(2):
                 cols = slice(h * HALF, (h + 1) * HALF)
                 quantize(x_grouped[h], x_codes[a][:, cols], x_scales[a][:, cols])
             if a == 0:
-                for m in range(6):
+                for m in range(4):
                     multiply(a, m)
 
         def finish(m):
@@ -159,15 +163,21 @@ def tile_list_heads_silu_kernel(tc, xT, w, wgt, b, offs, out):
         quantize_w(second, 1, 256, 256)
         finish(2)
         finish(3)
+        high = group_w(nc.vector.tensor_copy, 0, 512, 512, 256)
+        pieces = [group_w(nc.vector.tensor_copy, 1, 512, n0, P) for n0 in (512, 640)]
+        quantize_w(high, 0, 512, 256)
+        quantize_w(pieces[0], 1, 512, P)
+        quantize_w(pieces[1], 1, 640, P)
+        for m in (4, 5):
+            multiply(0, m)
+        finish(4)
+        finish(5)
         last = group_w(nc.vector.tensor_copy, 0, 768, 768, 256)
-        for n0 in (512, 768):
-            pieces = [group_w(nc.vector.tensor_copy, 1, n0, n0 + c, P) for c in (0, P)]
-            if n0 == 512:
-                quantize_w(last, 0, 768, 256)
-            for c in (0, 1):
-                quantize_w(pieces[c], 1, n0 + c * P, P)
-            if n0 == 768:
-                multiply(0, 6)
-                multiply(0, 7)
-            finish(n0 // P)
-            finish(n0 // P + 1)
+        pieces = [group_w(nc.vector.tensor_copy, 1, 768, 768, P)]
+        quantize_w(last, 0, 768, 256)
+        quantize_w(pieces[0], 1, 768, P)
+        for m in (6, 7):
+            multiply(0, m)
+        finish(6)
+        quantize_w(group_w(nc.vector.tensor_copy, 1, 896, 896, P), 1, 896, P)
+        finish(7)

from contextlib import ExitStack

import concourse.mybir as mybir

K, M, T, S = 1024, 1024, 2048, 512
FLOPS = 2 * K * M * S

F32 = mybir.dt.float32
BF16 = mybir.dt.bfloat16
U16 = mybir.dt.uint16
U32 = mybir.dt.uint32
U8 = mybir.dt.uint8
FP8X4 = mybir.dt.float8_e4m3fn_x4
MULT = mybir.AluOpType.mult
SILU = mybir.ActivationFunctionType.Silu

P = 128
PACK = 4
PASSES = K // (P * PACK)
HALF = S // 2
N_TILES = M // P


def tile_list_heads_silu_kernel(tc, xT, w, wgt, b, offs, out):
    nc = tc.nc
    with ExitStack() as ctx:
        keep = ctx.enter_context(tc.tile_pool(name="keep", bufs=1))
        psum = ctx.enter_context(tc.psum_pool(name="psum", bufs=1))

        offsets = keep.tile([P, S // 16], U16, name="offsets")
        nc.sync.dma_start(offsets[:], offs)

        x_rows = xT.rearrange("(a p i) t -> a i p t", p=P, i=PACK)
        w_rows = w.rearrange("(a p i) n -> a p i n", p=P, i=PACK)

        w_raw = {}

        def load_w(a, n0, width):
            raw = keep.tile([P, PACK, width], F32, name=f"w_raw_{a}_{n0}")
            nc.sync.dma_start(raw[:], w_rows[a][:, :, n0 : n0 + width])
            w_raw[(a, n0)] = raw

        x_planes = {}

        def load_x(a, i):
            plane = keep.tile([P, T], F32, name=f"x_{a}_{i}")
            nc.sync.dma_start(plane[:], x_rows[a, i])
            x_planes[(a, i)] = plane

        load_w(0, 0, 512)

        b_rows = keep.tile([P, 32], F32, name="b_rows", align_bytes=64)
        bias = keep.tile([P, 32], F32, name="bias", align_bytes=64)
        nc.vector.memset(b_rows[:], 0.0)
        b_view = b.rearrange("(c q r) -> q c r", q=4, r=32)
        for q in range(4):
            nc.sync.dma_start(b_rows[32 * q : 32 * q + N_TILES, :], b_view[q])
        weights = keep.tile([P, S], F32, name="weights")
        nc.sync.dma_start(weights[:], wgt)
        load_w(1, 0, 256)
        for a in range(PASSES):
            for i in range(PACK):
                load_x(a, i)
        for a, n0, width in ((1, 256, 256), (0, 512, 256), (1, 512, 256), (0, 768, 256), (1, 768, 128), (1, 896, 128)):
            load_w(a, n0, width)

        warm = keep.tile([P, 1], F32, name="warm")
        nc.vector.memset(warm[:], 0.0)
        nc.scalar.activation(warm[:], warm[:], SILU)

        def interleave(copy, grouped, source):
            copy(
                out=grouped[:].rearrange("p (c e) i -> p c i e", e=4),
                in_=source.rearrange("p i (c e) -> p c i e", e=4),
            )

        def quantize(grouped, codes, scales):
            nc.vector.quantize_mx(
                out=codes.bitcast(FP8X4), scales=scales, in_=grouped[:].rearrange("p n i -> p (n i)")
            )

        w_tiles = {}

        def group_w(copy, a, raw_n0, n0, width):
            grouped = keep.tile([P, width, PACK], BF16, name=f"w_grouped_{a}_{n0}", align_bytes=64)
            start = n0 - raw_n0
            interleave(copy, grouped, w_raw[(a, raw_n0)][:, :, start : start + width])
            return grouped

        def quantize_w(grouped, a, n0, width):
            codes = keep.tile([P, width], U32, name=f"w_codes_{a}_{n0}", align_bytes=64)
            scales = keep.tile([P, width], U8, name=f"w_scales_{a}_{n0}", align_bytes=64)
            quantize(grouped, codes[:], scales[:])
            for c in range(0, width, P):
                w_tiles[(a, (n0 + c) // P)] = (codes[:, c : c + P], scales[:, c : c + P])

        low = group_w(nc.scalar.copy, 0, 0, 0, 512)
        first = group_w(nc.scalar.copy, 1, 0, 0, 256)
        quantize_w(low, 0, 0, 512)
        quantize_w(first, 1, 0, 256)

        nc.vector.transpose(bias[:], b_rows[:])

        acc = [psum.tile([P, S], F32, name=f"acc_{m}") for m in range(N_TILES)]
        x_codes = [keep.tile([P, S], U32, name=f"x_codes_{a}", align_bytes=64) for a in range(PASSES)]
        x_scales = [keep.tile([P, S], U8, name=f"x_scales_{a}", align_bytes=64) for a in range(PASSES)]
        picked = {}

        def gather(a, i, h):
            nc.vector.tensor_tensor(
                picked[(a, h)][:, i, :],
                x_planes[(a, i)][:].indirect(offsets[:, h * (HALF // 16) : (h + 1) * (HALF // 16)]),
                weights[:, h * HALF : (h + 1) * HALF],
                MULT,
            )

        def multiply(a, m):
            codes, scales = w_tiles[(a, m)]
            nc.tensor.matmul_mx(
                out=acc[m][:],
                lhsT=codes.bitcast(FP8X4),
                lhsT_scale=scales,
                rhs=x_codes[a][:].bitcast(FP8X4),
                rhs_scale=x_scales[a][:],
                start=(a == 0),
                stop=(a == PASSES - 1),
            )

        for a in range(PASSES):
            for h in range(2):
                picked[(a, h)] = keep.tile([P, PACK, HALF], F32, name=f"picked_{a}_{h}")
            x_grouped = [
                keep.tile([P, HALF, PACK], BF16, name=f"x_grouped_{a}_{h}", align_bytes=64) for h in range(2)
            ]
            for i in range(PACK):
                for h in range(2):
                    gather(a, i, h)
                if a == 1 and i % 2 == 1:
                    for h, copy in ((0, nc.scalar.copy), (1, nc.vector.tensor_copy)):
                        copy(
                            out=x_grouped[h][:, :, i - 1 : i + 1],
                            in_=picked[(a, h)][:, i - 1 : i + 1, :].rearrange("p i j -> p j i"),
                        )
            if a == 0:
                for h in range(2):
                    interleave(nc.scalar.copy, x_grouped[h], picked[(a, h)][:])
            for h in range(2):
                cols = slice(h * HALF, (h + 1) * HALF)
                quantize(x_grouped[h], x_codes[a][:, cols], x_scales[a][:, cols])
            if a == 0:
                for m in range(4):
                    multiply(a, m)

        def finish(m):
            multiply(1, m)
            result = keep.tile([P, S], F32, name=f"result_{m}")
            nc.scalar.activation(result[:], acc[m][:], SILU, bias=bias[:, m : m + 1])
            nc.sync.dma_start(out[m * P : (m + 1) * P, :], result[:])

        second = group_w(nc.scalar.copy, 1, 256, 256, 256)
        finish(0)
        finish(1)
        quantize_w(second, 1, 256, 256)
        finish(2)
        finish(3)
        high = group_w(nc.vector.tensor_copy, 0, 512, 512, 256)
        pieces = [group_w(nc.vector.tensor_copy, 1, 512, n0, P) for n0 in (512, 640)]
        quantize_w(high, 0, 512, 256)
        quantize_w(pieces[0], 1, 512, P)
        quantize_w(pieces[1], 1, 640, P)
        for m in (4, 5):
            multiply(0, m)
        finish(4)
        finish(5)
        last = group_w(nc.vector.tensor_copy, 0, 768, 768, 256)
        pieces = [group_w(nc.vector.tensor_copy, 1, 768, 768, P)]
        quantize_w(last, 0, 768, 256)
        quantize_w(pieces[0], 1, 768, P)
        for m in (6, 7):
            multiply(0, m)
        finish(6)
        quantize_w(group_w(nc.vector.tensor_copy, 1, 896, 896, P), 1, 896, P)
        finish(7)
